import numpy as np
import ml_dtypes


def mxq(x, axis, fmt="e4m3"):
    dtype, down = {"e4m3": (ml_dtypes.float8_e4m3fn, 7), "e5m2": (ml_dtypes.float8_e5m2, 14)}[fmt]
    v = np.moveaxis(np.asarray(x, np.float32).astype(ml_dtypes.bfloat16).astype(np.float64), axis, -1)
    blocks = v.reshape(v.shape[:-1] + (-1, 32))
    amax = np.abs(blocks).max(-1, keepdims=True)
    byte = np.maximum(np.where(amax > 0, np.frexp(amax)[1] - 1 + 127, 0) - down, 1)
    scale = np.exp2(byte - 127.0)
    codes = (blocks / scale).astype(np.float32).astype(dtype).astype(np.float64)
    return np.moveaxis((codes * scale).reshape(v.shape), -1, axis)


WIDE = False


def mx_kscale(k):
    if not WIDE:
        return np.ones(k)
    levels = np.array([10, -10, 5, -5, 0])
    if k % 512:
        return np.exp2(np.random.permutation(np.resize(levels, k // 32))).repeat(32)
    a = np.empty((k // 512, 16))
    for p in range(k // 512):
        a[p, :8] = np.random.permutation(np.resize(levels, 8))
        for g in range(8):
            far = levels[np.abs(levels - a[p, g]) >= 10]
            a[p, g + 8] = far[np.random.randint(len(far))]
    return np.exp2(a.ravel()).repeat(32)


def f64(x):
    return np.asarray(x).astype(np.float64)


def striped(idx):
    return np.tile(idx.reshape(-1, 16).T, (8, 1)).astype(np.uint16)


def unstriped(offs):
    return offs[:16].T.reshape(-1).astype(np.int64)


def pack_weight(w):
    k, n = w.shape
    w = f64(np.asarray(w, np.float32).astype(ml_dtypes.bfloat16)).reshape(k // 32, 32, n)
    amax = np.abs(w).max(1)
    byte = np.clip(np.where(amax > 0, np.frexp(amax)[1] - 1 + 127 - 7, 1), 1, 254)
    scaled = (w * np.exp2(127.0 - byte)[:, None, :]).reshape(k, n).astype(np.float32)
    words = np.ascontiguousarray(scaled.reshape(k // 512, 128, 4, n).transpose(0, 1, 3, 2)).astype(ml_dtypes.float8_e4m3fn).view(np.uint8)
    return words, np.ascontiguousarray(byte.astype(np.uint8).reshape(k // 512, 16, n))


def unpack_weight(words, scales):
    g, p, n, _ = words.shape
    vals = np.ascontiguousarray(words).view(ml_dtypes.float8_e4m3fn).astype(np.float64) * np.repeat(np.exp2(scales.astype(np.float64) - 127.0), 8, axis=1)[..., None]
    return vals.transpose(0, 1, 3, 2).reshape(g * 512, n)


E2M1 = np.array([0.0, 0.5, 1.0, 1.5, 2.0, 3.0, 4.0, 6.0, -0.0, -0.5, -1.0, -1.5, -2.0, -3.0, -4.0, -6.0])


def pack_fp4(w):
    k, n = w.shape
    w = f64(np.asarray(w, np.float32).astype(ml_dtypes.bfloat16)).reshape(k // 32, 32, n)
    amax = np.abs(w).max(1)
    mant, ex = np.frexp(amax / 6.0)
    byte = np.clip(np.where(amax > 0, np.where(mant > 0.5, ex, ex - 1) + 127, 1), 1, 254)
    scaled = (w * np.exp2(127.0 - byte)[:, None, :]).reshape(k, n).astype(np.float32)
    c = np.ascontiguousarray(scaled.reshape(k // 512, 128, 4, n).transpose(0, 1, 3, 2)).astype(ml_dtypes.float4_e2m1fn).view(np.uint8) & 0xF
    words = (c[..., 0::2] | (c[..., 1::2] << 4)).reshape(k // 512, 128, 2 * n)
    return np.ascontiguousarray(words), np.ascontiguousarray(byte.astype(np.uint8).reshape(k // 512, 16, n))


def unpack_fp4(words, scales):
    g, _, n = scales.shape
    words = np.ascontiguousarray(words).reshape(g, 128, n, 2)
    nib = np.empty((g, 128, n, 4), np.uint8)
    nib[..., 0::2] = words & 0xF
    nib[..., 1::2] = words >> 4
    vals = E2M1[nib] * np.repeat(np.exp2(scales.astype(np.float64) - 127.0), 8, axis=1)[..., None]
    return vals.transpose(0, 1, 3, 2).reshape(g * 512, n)


def relu(v):
    return np.maximum(v, 0.0)


def sigmoid(v):
    return 1.0 / (1.0 + np.exp(-np.maximum(v, -700.0)))


K, T, S, D, N, H, V, U = 512, 4096, 1024, 4, 256, 512, 256, 512


def setup_inputs():
    n = np.random.standard_normal
    s = mx_kscale(K)[:, None]
    u = mx_kscale(H)
    packed_xT = pack_weight(n((K, T)) * s)
    packed_w1 = pack_fp4(n((K, H)) / np.sqrt(K) / s)
    packed_w2 = pack_fp4(n((K, H)) / np.sqrt(K) / s)
    packed_w3 = pack_fp4(n((H, N)) / np.sqrt(H) / u[:, None])
    return {
        "x_words": packed_xT[0],
        "x_scales": packed_xT[1],
        "w1_words": packed_w1[0],
        "w1_scales": packed_w1[1],
        "w2_words": packed_w2[0],
        "w2_scales": packed_w2[1],
        "qry": (n((H, U))).astype(np.float32),
        "unit": (np.random.uniform(0.6, 1.4, (H, 1)) * u[:, None]).astype(np.float32),
        "w3_words": packed_w3[0],
        "w3_scales": packed_w3[1],
        "old": (n((N, U))).astype(np.float32),
        "offs": striped(np.random.permutation(T)[:S]),
        "pg": striped(np.random.permutation(np.concatenate([np.arange(V), np.random.randint(0, V, U - V)]))),
    }


def reference(x_words, x_scales, w1_words, w1_scales, w2_words, w2_scales, qry, unit, w3_words, w3_scales, old, offs, pg):
    xq = unpack_weight(x_words, x_scales)[:, unstriped(offs)]
    yw = unpack_fp4(w2_words, w2_scales).T @ xq
    ys = unpack_fp4(w1_words, w1_scales).T @ xq
    sc = sigmoid(yw) * relu(ys)
    best = sc.reshape(len(sc), -1, D).max(axis=2)
    tp = best[:, unstriped(pg)]
    mt = tp * (np.tanh(f64(qry)))
    hid = f64(unit) * (mt - (np.repeat(mt.reshape(len(mt), -1, D).mean(axis=2), D, axis=1)))
    rr = unpack_fp4(w3_words, w3_scales).T @ mxq(hid, 0, "e4m3")
    return rr + f64(old)

@@ -1,0 +1,240 @@
+from contextlib import ExitStack
+
+import concourse.mybir as mybir
+
+K, T, S, D, N, H, V, U = 512, 4096, 1024, 4, 256, 512, 256, 512
+FLOPS = 2 * (2 * K * H * S + H * N * U)
+
+F32 = mybir.dt.float32
+BF16 = mybir.dt.bfloat16
+I32 = mybir.dt.int32
+U32 = mybir.dt.uint32
+U16 = mybir.dt.uint16
+U8 = mybir.dt.uint8
+FP8X4 = mybir.dt.float8_e4m3fn_x4
+FP4X4 = mybir.dt.float4_e2m1fn_x4
+ACT = mybir.ActivationFunctionType
+ALU = mybir.AluOpType
+
+P = 128
+PACK = 4
+BANK = 512
+HALF = U // 2
+
+
+def load_scale_rows(queues, plane, scales):
+    for q, queue in enumerate(queues):
+        queue.dma_start(
+            out=plane[32 * q : 32 * q + 4, :].bitcast(I32),
+            in_=scales[0, 4 * q : 4 * q + 4, :].bitcast(I32),
+        )
+
+
+def tile_picked_yxindx_cent_p_kernel(
+    tc, x_words, x_scales, w1_words, w1_scales, w2_words, w2_scales, qry, unit, w3_words, w3_scales, old, offs, pg, out
+):
+    nc = tc.nc
+    with ExitStack() as ctx:
+        lists = ctx.enter_context(tc.tile_pool(name="lists", bufs=1))
+        keep = ctx.enter_context(tc.tile_pool(name="keep", bufs=1))
+        ring = ctx.enter_context(tc.tile_pool(name="ring", bufs=2))
+        psum = ctx.enter_context(tc.psum_pool(name="psum", bufs=1))
+
+        offs_t = lists.tile([P, S // 16], U16, name="offs_t")
+        pg_t = lists.tile([P, U // 16], U16, name="pg_t")
+
+        w2s_raw = keep.tile([P, H], U8, name="w2s_raw", tag="late_old", align_bytes=64)
+        w1s_raw = keep.tile([P, H], U8, name="w1s_raw", tag="late_w3s", align_bytes=64)
+        xs_win = keep.tile([P, T], U8, name="xs_win", tag="late_w3w", align_bytes=64)
+        xw_win = keep.tile([P, T], U32, name="xw_win", align_bytes=64)
+        w2w_raw = keep.tile([P, 2 * H], U8, name="w2w_raw", tag="late_qa", align_bytes=64)
+        w1w_raw = keep.tile([P, 2 * H], U8, name="w1w_raw", tag="late_qb", align_bytes=64)
+
+        nc.vector.memset(xs_win[:].bitcast(I32), 0)
+        nc.vector.memset(w2s_raw[:].bitcast(I32), 0)
+        nc.gpsimd.memset(w1s_raw[:].bitcast(I32), 0)
+
+        nc.sync.dma_start(offs_t[:], offs)
+        nc.sync.dma_start(out=w2w_raw[:].bitcast(I32), in_=w2_words[0].bitcast(I32))
+        nc.sync.dma_start(out=w1w_raw[:].bitcast(I32), in_=w1_words[0].bitcast(I32))
+        nc.sync.dma_start(pg_t[:], pg)
+        nc.sync.dma_start(out=xw_win[:].bitcast(I32), in_=x_words[0].rearrange("p n t -> p (n t)").bitcast(I32))
+        load_scale_rows([nc.scalar] * 4, xs_win, x_scales)
+        load_scale_rows([nc.gpsimd] * 4, w1s_raw, w1_scales)
+        load_scale_rows([nc.scalar] * 3 + [nc.gpsimd], w2s_raw, w2_scales)
+
+        warm = keep.tile([P, 1], F32, name="warm")
+        warm_out = keep.tile([P, 1], F32, name="warm_out")
+        nc.vector.memset(warm[:], 0.0)
+        nc.scalar.activation(out=warm_out[:], in_=warm[:], func=ACT.Sigmoid)
+
+        def deal_words(raw, name):
+            dealt = keep.tile([P, PACK, 2 * P], U8, name=name, align_bytes=64)
+            nc.vector.tensor_copy(
+                out=dealt[:].rearrange("p t (m b) -> p t m b", b=2),
+                in_=raw[:].rearrange("p (m t b) -> p t m b", t=PACK, b=2),
+            )
+            return dealt
+
+        def deal_scales(raw, name):
+            dealt = keep.tile([P, PACK, P], U8, name=name, align_bytes=64)
+            nc.vector.tensor_copy(out=dealt[:], in_=raw[:].rearrange("p (m t) -> p t m", t=PACK))
+            return dealt
+
+        w2w = deal_words(w2w_raw, "w2w")
+        w1w = deal_words(w1w_raw, "w1w")
+        xs = keep.tile([P, S], U8, name="xs", align_bytes=64)
+        nc.vector.tensor_copy(out=xs[:], in_=xs_win[:].indirect(offs_t[:]))
+        w2s = deal_scales(w2s_raw, "w2s")
+        xw = []
+        for h in range(2):
+            xw_h = keep.tile([P, BANK], U32, name="xw%d" % h, align_bytes=64)
+            nc.vector.tensor_copy(out=xw_h[:], in_=xw_win[:].indirect(offs_t[:, 32 * h : 32 * h + 32]))
+            xw.append(xw_h)
+        w1s = deal_scales(w1s_raw, "w1s")
+
+        qry_v = qry.rearrange("(p t) r -> p t r", t=PACK)
+        q_first = keep.tile([P, 2 * U + PACK], F32, name="q_first", tag="late_qa", align_bytes=64)
+        q_second = keep.tile([P, 2 * U], F32, name="q_second", tag="late_qb", align_bytes=64)
+        nc.sync.dma_start(out=q_first[:, 0 : 2 * U].rearrange("p (t r) -> p t r", t=2), in_=qry_v[:, 0:2, :])
+        unit_t = q_first[:, 2 * U :]
+        nc.sync.dma_start(out=unit_t, in_=unit.rearrange("(p t) o -> p (t o)", t=PACK))
+        nc.sync.dma_start(out=q_second[:].rearrange("p (t r) -> p t r", t=2), in_=qry_v[:, 2:4, :])
+        q_tiles = [q_first, q_second]
+        old_t = keep.tile([P, 2, U], F32, name="old_t", tag="late_old", align_bytes=64)
+        nc.sync.dma_start(out=old_t[:], in_=old.rearrange("(m p) r -> p m r", p=P))
+        w3w = keep.tile([P, 2 * N], U8, name="w3w", tag="late_w3w", align_bytes=64)
+        nc.sync.dma_start(out=w3w[:].bitcast(I32), in_=w3_words[0].bitcast(I32))
+        w3s = keep.tile([P, N], U8, name="w3s", tag="late_w3s", align_bytes=64)
+        nc.vector.memset(w3s[:].bitcast(I32), 0)
+        load_scale_rows([nc.sync] * 4, w3s, w3_scales)
+
+        mt = keep.tile([P, PACK, U], F32, name="mt")
+        pair_sum = keep.tile([P, PACK, U // 2], F32, name="pair_sum")
+        group_sum = keep.tile([P, PACK, U // D], F32, name="group_sum")
+        prods, wins, factors = {}, {}, {}
+
+        def product(words, scales, t, h, tag):
+            acc = psum.tile([P, BANK], F32, name=tag, tag=tag, bufs=3)
+            nc.tensor.matmul_mx(
+                out=acc[:],
+                lhsT=words[:, t, :].bitcast(FP4X4),
+                lhsT_scale=scales[:, t, :],
+                rhs=xw[h][:].bitcast(FP8X4),
+                rhs_scale=xs[:, BANK * h : BANK * (h + 1)],
+                start=True,
+                stop=True,
+            )
+            return acc
+
+        def score(t, h):
+            if h == 0:
+                prods[t] = ring.tile([P, S], F32, name="prod")
+            yw = product(w2w, w2s, t, h, "yw")
+            ys = product(w1w, w1s, t, h, "ys")
+            gate = ring.tile([P, BANK], F32, name="gate", bufs=3)
+            nc.scalar.activation(out=gate[:], in_=yw[:], func=ACT.Sigmoid)
+            nc.vector.scalar_tensor_tensor(
+                out=prods[t][:, BANK * h : BANK * (h + 1)], in0=ys[:], scalar=0.0, in1=gate[:], op0=ALU.max, op1=ALU.mult
+            )
+
+        def factor(t):
+            th = ring.tile([P, U], F32, name="th")
+            nc.scalar.activation(out=th[:], in_=q_tiles[t // 2][:, (t % 2) * U : (t % 2 + 1) * U], func=ACT.Tanh)
+            factors[t] = ring.tile([P, U], F32, name="fac")
+            nc.scalar.activation(out=factors[t][:], in_=th[:], func=ACT.Copy, scale=unit_t[:, t : t + 1])
+
+        def max_pairs(t):
+            wins[t] = ring.tile([P, V + 2 * V], F32, name="win")
+            quads = prods[t][:].rearrange("p (v d) -> p v d", d=D)
+            nc.vector.tensor_tensor(
+                out=wins[t][:, V:].rearrange("p (v e) -> p v e", e=2), in0=quads[:, :, 0:2], in1=quads[:, :, 2:4], op=ALU.max
+            )
+
+        def max_final(t):
+            pairs = wins[t][:, V:].rearrange("p (v e) -> p v e", e=2)
+            nc.vector.tensor_tensor(out=wins[t][:, 0:V], in0=pairs[:, :, 0], in1=pairs[:, :, 1], op=ALU.max)
+
+        def look_up(t, lo, hi):
+            nc.vector.tensor_tensor(
+                out=mt[:, t, lo:hi], in0=wins[t][:].indirect(pg_t[:, lo // 16 : hi // 16]), in1=factors[t][:, lo:hi], op=ALU.mult
+            )
+
+        def sum_pairs(t, lo, hi):
+            quads = mt[:, t, lo:hi].rearrange("p (g d) -> p g d", d=D)
+            nc.vector.tensor_tensor(
+                out=pair_sum[:, t, lo // 2 : hi // 2].rearrange("p (g e) -> p g e", e=2),
+                in0=quads[:, :, 0:2], in1=quads[:, :, 2:4], op=ALU.add,
+            )
+
+        def sum_final(t, lo, hi):
+            pairs = pair_sum[:, t, lo // 2 : hi // 2].rearrange("p (g e) -> p g e", e=2)
+            nc.vector.tensor_tensor(out=group_sum[:, t, lo // D : hi // D], in0=pairs[:, :, 0], in1=pairs[:, :, 1], op=ALU.add)
+
+        last = PACK - 1
+        score(0, 0)
+        score(0, 1)
+        factor(0)
+        score(1, 0)
+        max_pairs(0)
+        for t in range(last):
+            score(t + 1, 1)
+            factor(t + 1)
+            max_final(t)
+            if t > 0:
+                sum_final(t - 1, 0, U)
+            max_pairs(t + 1)
+            look_up(t, 0, U)
+            if t + 2 <= last:
+                score(t + 2, 0)
+            else:
+                max_final(last)
+            sum_pairs(t, 0, U)
+        halves = [(h * HALF, (h + 1) * HALF) for h in range(2)]
+        for lo, hi in halves:
+            look_up(last, lo, hi)
+        sum_final(last - 1, 0, U)
+        for lo, hi in halves:
+            sum_pairs(last, lo, hi)
+        for lo, hi in halves:
+            sum_final(last, lo, hi)
+        means, hids = [], []
+        for lo, hi in halves:
+            mean = ring.tile([P, PACK, HALF // D], F32, name="mean")
+            nc.vector.tensor_scalar(
+                out=mean[:], in0=group_sum[:, :, lo // D : hi // D], scalar1=1.0 / D, scalar2=None, op0=ALU.mult
+            )
+            means.append(mean)
+        for h, (lo, hi) in enumerate(halves):
+            hid = ring.tile([P, HALF, PACK], BF16, name="hid", align_bytes=64)
+            nc.vector.tensor_tensor(
+                out=hid[:].rearrange("p (g d) t -> p g t d", d=D),
+                in0=mt[:, :, lo:hi].rearrange("p t (g d) -> p g t d", d=D),
+                in1=means[h][:].rearrange("p t g -> p g t").unsqueeze(3).to_broadcast([P, HALF // D, PACK, D]),
+                op=ALU.subtract,
+            )
+            hids.append(hid)
+        accs = []
+        for h in range(2):
+            codes = ring.tile([P, HALF], U32, name="codes", align_bytes=64)
+            plane = ring.tile([P, HALF], U8, name="plane", align_bytes=64)
+            nc.vector.quantize_mx(
+                out=codes[:].bitcast(FP8X4), scales=plane[:], in_=hids[h][:].rearrange("p r t -> p (r t)")
+            )
+            acc = psum.tile([P, 2, HALF], F32, name="rr", tag="rr", bufs=2)
+            for m in range(N // P):
+                nc.tensor.matmul_mx(
+                    out=acc[:, m, :],
+                    lhsT=w3w[:, 2 * P * m : 2 * P * (m + 1)].bitcast(FP4X4),
+                    lhsT_scale=w3s[:, P * m : P * (m + 1)],
+                    rhs=codes[:].bitcast(FP8X4),
+                    rhs_scale=plane[:],
+                    start=True,
+                    stop=True,
+                )
+            accs.append(acc)
+        out_v = out.rearrange("(m p) r -> p m r", p=P)
+        for h, (lo, hi) in enumerate(halves):
+            res = ring.tile([P, 2, HALF], F32, name="res")
+            nc.vector.tensor_tensor(out=res[:], in0=accs[h][:], in1=old_t[:, :, lo:hi], op=ALU.add)
+            nc.sync.dma_start(out=out_v[:, :, lo:hi], in_=res[:])

@@ -1,6 +1,7 @@
 from contextlib import ExitStack
 
 import concourse.mybir as mybir
+from concourse.masks import make_identity
 
 K, T, S, D, N, H, V, U = 512, 4096, 1024, 4, 256, 512, 256, 512
 FLOPS = 2 * (2 * K * H * S + H * N * U)
@@ -43,30 +44,31 @@ def tile_picked_yxindx_cent_p_kernel(
         offs_t = lists.tile([P, S // 16], U16, name="offs_t")
         pg_t = lists.tile([P, U // 16], U16, name="pg_t")
 
-        w2s_raw = keep.tile([P, H], U8, name="w2s_raw", tag="late_old", align_bytes=64)
-        w1s_raw = keep.tile([P, H], U8, name="w1s_raw", tag="late_w3s", align_bytes=64)
+        ws_raw = keep.tile([P, 2, H], U8, name="ws_raw", tag="late_old", align_bytes=64)
         xs_win = keep.tile([P, T], U8, name="xs_win", tag="late_w3w", align_bytes=64)
-        xw_win = keep.tile([P, T], U32, name="xw_win", align_bytes=64)
+        xw_win = keep.tile([P, T], U32, name="xw_win", tag="late_w3s", align_bytes=64)
         w2w_raw = keep.tile([P, 2 * H], U8, name="w2w_raw", tag="late_qa", align_bytes=64)
         w1w_raw = keep.tile([P, 2 * H], U8, name="w1w_raw", tag="late_qb", align_bytes=64)
 
-        nc.vector.memset(xs_win[:].bitcast(I32), 0)
-        nc.vector.memset(w2s_raw[:].bitcast(I32), 0)
-        nc.gpsimd.memset(w1s_raw[:].bitcast(I32), 0)
-
-        nc.sync.dma_start(offs_t[:], offs)
-        nc.sync.dma_start(out=w2w_raw[:].bitcast(I32), in_=w2_words[0].bitcast(I32))
-        nc.sync.dma_start(out=w1w_raw[:].bitcast(I32), in_=w1_words[0].bitcast(I32))
-        nc.sync.dma_start(pg_t[:], pg)
-        nc.sync.dma_start(out=xw_win[:].bitcast(I32), in_=x_words[0].rearrange("p n t -> p (n t)").bitcast(I32))
-        load_scale_rows([nc.scalar] * 4, xs_win, x_scales)
-        load_scale_rows([nc.gpsimd] * 4, w1s_raw, w1_scales)
-        load_scale_rows([nc.scalar] * 3 + [nc.gpsimd], w2s_raw, w2_scales)
-
+        nc.vector.memset(xs_win[:, 0 : T // 2].bitcast(I32), 0)
+        nc.gpsimd.memset(xs_win[:, T // 2 :].bitcast(I32), 0)
         warm = keep.tile([P, 1], F32, name="warm")
         warm_out = keep.tile([P, 1], F32, name="warm_out")
         nc.vector.memset(warm[:], 0.0)
         nc.scalar.activation(out=warm_out[:], in_=warm[:], func=ACT.Sigmoid)
+
+        nc.vector.memset(ws_raw[:].bitcast(I32), 0)
+        ident = keep.tile([P, P], F32, name="ident")
+        make_identity(nc, ident[:])
+
+        nc.sync.dma_start(offs_t[:], offs)
+        nc.sync.dma_start(out=w2w_raw[:].bitcast(I32), in_=w2_words[0].bitcast(I32))
+        nc.sync.dma_start(out=w1w_raw[:].bitcast(I32), in_=w1_words[0].bitcast(I32))
+        load_scale_rows([nc.sync] * 4, xs_win[:], x_scales)
+        nc.sync.dma_start(out=xw_win[:].bitcast(I32), in_=x_words[0].rearrange("p n t -> p (n t)").bitcast(I32))
+        load_scale_rows([nc.sync] * 4, ws_raw[:, 0, :], w2_scales)
+        load_scale_rows([nc.sync] * 3 + [nc.scalar], ws_raw[:, 1, :], w1_scales)
+        nc.sync.dma_start(pg_t[:], pg)
 
         def deal_words(raw, name):
             dealt = keep.tile([P, PACK, 2 * P], U8, name=name, align_bytes=64)
@@ -76,22 +78,22 @@ def tile_picked_yxindx_cent_p_kernel(
             )
             return dealt
 
-        def deal_scales(raw, name):
-            dealt = keep.tile([P, PACK, P], U8, name=name, align_bytes=64)
-            nc.vector.tensor_copy(out=dealt[:], in_=raw[:].rearrange("p (m t) -> p t m", t=PACK))
-            return dealt
-
         w2w = deal_words(w2w_raw, "w2w")
         w1w = deal_words(w1w_raw, "w1w")
         xs = keep.tile([P, S], U8, name="xs", align_bytes=64)
         nc.vector.tensor_copy(out=xs[:], in_=xs_win[:].indirect(offs_t[:]))
-        w2s = deal_scales(w2s_raw, "w2s")
-        xw = []
-        for h in range(2):
-            xw_h = keep.tile([P, BANK], U32, name="xw%d" % h, align_bytes=64)
-            nc.vector.tensor_copy(out=xw_h[:], in_=xw_win[:].indirect(offs_t[:, 32 * h : 32 * h + 32]))
-            xw.append(xw_h)
-        w1s = deal_scales(w1s_raw, "w1s")
+
+
+        def gather_words(h, tag):
+            picked = keep.tile([P, BANK], U32, name="xw%d" % h, tag=tag, align_bytes=64)
+            nc.vector.tensor_copy(out=picked[:], in_=xw_win[:].indirect(offs_t[:, 32 * h : 32 * h + 32]))
+            return picked
+
+        xw = [gather_words(0, "xw0")]
+        ws = keep.tile([P, 2, PACK, P], U8, name="ws", align_bytes=64)
+        nc.vector.tensor_copy(out=ws[:], in_=ws_raw[:].rearrange("p w (m t) -> p w t m", t=PACK))
+        w2s, w1s = ws[:, 0], ws[:, 1]
+        xw.append(gather_words(1, "late_old"))
 
         qry_v = qry.rearrange("(p t) r -> p t r", t=PACK)
         q_first = keep.tile([P, 2 * U + PACK], F32, name="q_first", tag="late_qa", align_bytes=64)
@@ -101,17 +103,14 @@ def tile_picked_yxindx_cent_p_kernel(
         nc.sync.dma_start(out=unit_t, in_=unit.rearrange("(p t) o -> p (t o)", t=PACK))
         nc.sync.dma_start(out=q_second[:].rearrange("p (t r) -> p t r", t=2), in_=qry_v[:, 2:4, :])
         q_tiles = [q_first, q_second]
-        old_t = keep.tile([P, 2, U], F32, name="old_t", tag="late_old", align_bytes=64)
-        nc.sync.dma_start(out=old_t[:], in_=old.rearrange("(m p) r -> p m r", p=P))
         w3w = keep.tile([P, 2 * N], U8, name="w3w", tag="late_w3w", align_bytes=64)
         nc.sync.dma_start(out=w3w[:].bitcast(I32), in_=w3_words[0].bitcast(I32))
         w3s = keep.tile([P, N], U8, name="w3s", tag="late_w3s", align_bytes=64)
         nc.vector.memset(w3s[:].bitcast(I32), 0)
-        load_scale_rows([nc.sync] * 4, w3s, w3_scales)
+        load_scale_rows([nc.sync] * 4, w3s[:], w3_scales)
 
         mt = keep.tile([P, PACK, U], F32, name="mt")
-        pair_sum = keep.tile([P, PACK, U // 2], F32, name="pair_sum")
-        group_sum = keep.tile([P, PACK, U // D], F32, name="group_sum")
+        mean = keep.tile([P, PACK, U // D], F32, name="mean")
         prods, wins, factors = {}, {}, {}
 
         def product(words, scales, t, h, tag):
@@ -129,7 +128,7 @@ def tile_picked_yxindx_cent_p_kernel(
 
         def score(t, h):
             if h == 0:
-                prods[t] = ring.tile([P, S], F32, name="prod")
+                prods[t] = ring.tile([P, S], F32, name="prod", bufs=3)
             yw = product(w2w, w2s, t, h, "yw")
             ys = product(w1w, w1s, t, h, "ys")
             gate = ring.tile([P, BANK], F32, name="gate", bufs=3)
@@ -145,7 +144,7 @@ def tile_picked_yxindx_cent_p_kernel(
             nc.scalar.activation(out=factors[t][:], in_=th[:], func=ACT.Copy, scale=unit_t[:, t : t + 1])
 
         def max_pairs(t):
-            wins[t] = ring.tile([P, V + 2 * V], F32, name="win")
+            wins[t] = ring.tile([P, V + 2 * V], F32, name="win", bufs=3)
             quads = prods[t][:].rearrange("p (v d) -> p v d", d=D)
             nc.vector.tensor_tensor(
                 out=wins[t][:, V:].rearrange("p (v e) -> p v e", e=2), in0=quads[:, :, 0:2], in1=quads[:, :, 2:4], op=ALU.max
@@ -160,57 +159,69 @@ def tile_picked_yxindx_cent_p_kernel(
                 out=mt[:, t, lo:hi], in0=wins[t][:].indirect(pg_t[:, lo // 16 : hi // 16]), in1=factors[t][:, lo:hi], op=ALU.mult
             )
 
-        def sum_pairs(t, lo, hi):
-            quads = mt[:, t, lo:hi].rearrange("p (g d) -> p g d", d=D)
-            nc.vector.tensor_tensor(
-                out=pair_sum[:, t, lo // 2 : hi // 2].rearrange("p (g e) -> p g e", e=2),
-                in0=quads[:, :, 0:2], in1=quads[:, :, 2:4], op=ALU.add,
-            )
-
-        def sum_final(t, lo, hi):
-            pairs = pair_sum[:, t, lo // 2 : hi // 2].rearrange("p (g e) -> p g e", e=2)
-            nc.vector.tensor_tensor(out=group_sum[:, t, lo // D : hi // D], in0=pairs[:, :, 0], in1=pairs[:, :, 1], op=ALU.add)
+        def mean_by_transposes(t):
+            turned = psum.tile([P, P], F32, name="turned", tag="rr", bufs=2)
+            members = mt[:, t, :].rearrange("p (g d) -> p d g", d=D)
+            for d in range(D):
+                nc.tensor.matmul(
+                    out=turned[:], lhsT=members[:, d, :], rhs=ident[:], is_transpose=True, start=(d == 0), stop=(d == D - 1)
+                )
+            mean_turned = ring.tile([P, P], F32, name="mean_turned")
+            nc.scalar.activation(out=mean_turned[:], in_=turned[:], func=ACT.Copy, scale=1.0 / D)
+            back = psum.tile([P, P], F32, name="back", tag="rr", bufs=2)
+            nc.tensor.transpose(back[:], mean_turned[:], ident[:])
+            nc.scalar.copy(out=mean[:, t, :], in_=back[:])
 
         last = PACK - 1
-        score(0, 0)
-        score(0, 1)
-        factor(0)
-        score(1, 0)
-        max_pairs(0)
-        for t in range(last):
-            score(t + 1, 1)
-            factor(t + 1)
-            max_final(t)
-            if t > 0:
-                sum_final(t - 1, 0, U)
-            max_pairs(t + 1)
-            look_up(t, 0, U)
-            if t + 2 <= last:
-                score(t + 2, 0)
-            else:
-                max_final(last)
-            sum_pairs(t, 0, U)
         halves = [(h * HALF, (h + 1) * HALF) for h in range(2)]
+        score(0, 0)
+        score(1, 0)
+        factor(0)
+        score(0, 1)
+        score(1, 1)
+        max_pairs(0)
+        score(2, 0)
+        factor(1)
+        max_final(0)
+        max_pairs(1)
+        look_up(0, 0, U)
+        score(2, 1)
+        mean_by_transposes(0)
+        max_final(1)
+        score(3, 0)
+        factor(2)
+        look_up(1, 0, U)
+        max_pairs(2)
+        score(3, 1)
+        factor(3)
+        mean_by_transposes(1)
+        max_final(2)
+        max_pairs(3)
+        look_up(2, 0, U)
+        mean_by_transposes(2)
+        max_final(3)
+        old_t = keep.tile([P, 2, U], F32, name="old_t", tag="late_old", align_bytes=64)
+        nc.sync.dma_start(out=old_t[:], in_=old.rearrange("(m p) r -> p m r", p=P))
         for lo, hi in halves:
             look_up(last, lo, hi)
-        sum_final(last - 1, 0, U)
+        sums = []
         for lo, hi in halves:
-            sum_pairs(last, lo, hi)
-        for lo, hi in halves:
-            sum_final(last, lo, hi)
-        means, hids = [], []
-        for lo, hi in halves:
-            mean = ring.tile([P, PACK, HALF // D], F32, name="mean")
-            nc.vector.tensor_scalar(
-                out=mean[:], in0=group_sum[:, :, lo // D : hi // D], scalar1=1.0 / D, scalar2=None, op0=ALU.mult
+            total = ring.tile([P, HALF // D], F32, name="total")
+            nc.vector.tensor_reduce(
+                out=total[:], in_=mt[:, last, lo:hi].rearrange("p (g d) -> p g d", d=D), axis=mybir.AxisListType.X, op=ALU.add
             )
-            means.append(mean)
+            sums.append(total)
+        for h, (lo, hi) in enumerate(halves):
+            nc.vector.tensor_scalar(
+                out=mean[:, last, lo // D : hi // D], in0=sums[h][:], scalar1=1.0 / D, scalar2=None, op0=ALU.mult
+            )
+        hids = []
         for h, (lo, hi) in enumerate(halves):
             hid = ring.tile([P, HALF, PACK], BF16, name="hid", align_bytes=64)
             nc.vector.tensor_tensor(
                 out=hid[:].rearrange("p (g d) t -> p g t d", d=D),
                 in0=mt[:, :, lo:hi].rearrange("p t (g d) -> p g t d", d=D),
-                in1=means[h][:].rearrange("p t g -> p g t").unsqueeze(3).to_broadcast([P, HALF // D, PACK, D]),
+                in1=mean[:, :, lo // D : hi // D].rearrange("p t g -> p g t").unsqueeze(3).to_broadcast([P, HALF // D, PACK, D]),
                 op=ALU.subtract,
             )
             hids.append(hid)

@@ -24,11 +24,8 @@ HALF = U // 2
 
 
 def load_scale_rows(queues, plane, scales):
-    for q, queue in enumerate(queues):
-        queue.dma_start(
-            out=plane[32 * q : 32 * q + 4, :].bitcast(I32),
-            in_=scales[0, 4 * q : 4 * q + 4, :].bitcast(I32),
-        )
+    for r, queue in enumerate(queues):
+        queue.dma_start(out=plane[r:P:32, :].bitcast(I32), in_=scales[0, r:16:4, :].bitcast(I32))
 
 
 def tile_picked_yxindx_cent_p_kernel(
@@ -110,7 +107,7 @@ def tile_picked_yxindx_cent_p_kernel(
         load_scale_rows([nc.sync] * 4, w3s[:], w3_scales)
 
         mt = keep.tile([P, PACK, U], F32, name="mt")
-        mean = keep.tile([P, PACK, U // D], F32, name="mean")
+        mean = keep.tile([P, PACK, U], F32, name="mean")
         prods, wins, factors = {}, {}, {}
 
         def product(words, scales, t, h, tag):
@@ -170,35 +167,39 @@ def tile_picked_yxindx_cent_p_kernel(
             nc.scalar.activation(out=mean_turned[:], in_=turned[:], func=ACT.Copy, scale=1.0 / D)
             back = psum.tile([P, P], F32, name="back", tag="rr", bufs=2)
             nc.tensor.transpose(back[:], mean_turned[:], ident[:])
-            nc.scalar.copy(out=mean[:, t, :], in_=back[:])
+            for lo, hi in halves:
+                nc.scalar.copy(
+                    out=mean[:, t, lo:hi].rearrange("p (g d) -> p g d", d=D),
+                    in_=back[:, lo // D : hi // D].unsqueeze(2).to_broadcast([P, HALF // D, D]),
+                )
 
         last = PACK - 1
         halves = [(h * HALF, (h + 1) * HALF) for h in range(2)]
         score(0, 0)
         score(1, 0)
-        factor(0)
         score(0, 1)
         score(1, 1)
         max_pairs(0)
         score(2, 0)
-        factor(1)
+        factor(0)
         max_final(0)
         max_pairs(1)
         look_up(0, 0, U)
         score(2, 1)
+        factor(1)
         mean_by_transposes(0)
         max_final(1)
+        max_pairs(2)
+        look_up(1, 0, U)
         score(3, 0)
         factor(2)
-        look_up(1, 0, U)
-        max_pairs(2)
-        score(3, 1)
-        factor(3)
-        mean_by_transposes(1)
         max_final(2)
-        max_pairs(3)
+        score(3, 1)
+        mean_by_transposes(1)
         look_up(2, 0, U)
         mean_by_transposes(2)
+        factor(3)
+        max_pairs(3)
         max_final(3)
         old_t = keep.tile([P, 2, U], F32, name="old_t", tag="late_old", align_bytes=64)
         nc.sync.dma_start(out=old_t[:], in_=old.rearrange("(m p) r -> p m r", p=P))
@@ -213,15 +214,17 @@ def tile_picked_yxindx_cent_p_kernel(
             sums.append(total)
         for h, (lo, hi) in enumerate(halves):
             nc.vector.tensor_scalar(
-                out=mean[:, last, lo // D : hi // D], in0=sums[h][:], scalar1=1.0 / D, scalar2=None, op0=ALU.mult
+                out=mean[:, last, lo:hi].rearrange("p (g d) -> p g d", d=D),
+                in0=sums[h][:].unsqueeze(2).to_broadcast([P, HALF // D, D]),
+                scalar1=1.0 / D, scalar2=None, op0=ALU.mult,
             )
         hids = []
         for h, (lo, hi) in enumerate(halves):
             hid = ring.tile([P, HALF, PACK], BF16, name="hid", align_bytes=64)
             nc.vector.tensor_tensor(
-                out=hid[:].rearrange("p (g d) t -> p g t d", d=D),
-                in0=mt[:, :, lo:hi].rearrange("p t (g d) -> p g t d", d=D),
-                in1=mean[:, :, lo // D : hi // D].rearrange("p t g -> p g t").unsqueeze(3).to_broadcast([P, HALF // D, PACK, D]),
+                out=hid[:].rearrange("p (c e) t -> p c t e", e=2),
+                in0=mt[:, :, lo:hi].rearrange("p t (c e) -> p c t e", e=2),
+                in1=mean[:, :, lo:hi].rearrange("p t (c e) -> p c t e", e=2),
                 op=ALU.subtract,
             )
             hids.append(hid)
@@ -232,10 +235,10 @@ def tile_picked_yxindx_cent_p_kernel(
             nc.vector.quantize_mx(
                 out=codes[:].bitcast(FP8X4), scales=plane[:], in_=hids[h][:].rearrange("p r t -> p (r t)")
             )
-            acc = psum.tile([P, 2, HALF], F32, name="rr", tag="rr", bufs=2)
-            for m in range(N // P):
+            for m, tag in enumerate(("yw", "ys")):
+                acc = psum.tile([P, HALF], F32, name="rr", tag=tag, bufs=3)
                 nc.tensor.matmul_mx(
-                    out=acc[:, m, :],
+                    out=acc[:],
                     lhsT=w3w[:, 2 * P * m : 2 * P * (m + 1)].bitcast(FP4X4),
                     lhsT_scale=w3s[:, P * m : P * (m + 1)],
                     rhs=codes[:].bitcast(FP8X4),
@@ -243,9 +246,10 @@ def tile_picked_yxindx_cent_p_kernel(
                     start=True,
                     stop=True,
                 )
-            accs.append(acc)
-        out_v = out.rearrange("(m p) r -> p m r", p=P)
-        for h, (lo, hi) in enumerate(halves):
-            res = ring.tile([P, 2, HALF], F32, name="res")
-            nc.vector.tensor_tensor(out=res[:], in0=accs[h][:], in1=old_t[:, :, lo:hi], op=ALU.add)
-            nc.sync.dma_start(out=out_v[:, :, lo:hi], in_=res[:])
+                accs.append((h, m, acc))
+        for h, m, acc in accs:
+            lo, hi = halves[h]
+            res = ring.tile([P, HALF], F32, name="res", bufs=4)
+            nc.vector.tensor_tensor(out=res[:], in0=acc[:], in1=old_t[:, m, lo:hi], op=ALU.add)
+            queue = nc.sync if m == 0 else nc.scalar
+            queue.dma_start(out=out[P * m : P * (m + 1), lo:hi], in_=res[:])

@@ -18,14 +18,12 @@ ACT = mybir.ActivationFunctionType
 ALU = mybir.AluOpType
 
 P = 128
-PACK = 4
+PLANES = 4
+QUAD = 32
+SPREAD = 8
 BANK = 512
 HALF = U // 2
-
-
-def load_scale_rows(queues, plane, scales):
-    for r, queue in enumerate(queues):
-        queue.dma_start(out=plane[r:P:32, :].bitcast(I32), in_=scales[0, r:16:4, :].bitcast(I32))
+PER_COLUMN = 16
 
 
 def tile_picked_yxindx_cent_p_kernel(
@@ -38,126 +36,130 @@ def tile_picked_yxindx_cent_p_kernel(
         ring = ctx.enter_context(tc.tile_pool(name="ring", bufs=2))
         psum = ctx.enter_context(tc.psum_pool(name="psum", bufs=1))
 
-        offs_t = lists.tile([P, S // 16], U16, name="offs_t")
-        pg_t = lists.tile([P, U // 16], U16, name="pg_t")
+        offs_t = lists.tile([P, S // PER_COLUMN], U16, name="offs_t")
+        pg_t = lists.tile([P, U // PER_COLUMN], U16, name="pg_t")
+        ws_raw = keep.tile([P, 2, H], U8, name="ws_raw", tag="then_old", align_bytes=64)
+        xs_win = keep.tile([P, T], U8, name="xs_win", align_bytes=64)
+        xw_win = keep.tile([P, T], U32, name="xw_win", tag="then_qry_high", align_bytes=64)
+        w2w_raw = keep.tile([P, 2 * H], U8, name="w2w_raw", tag="then_w3w", align_bytes=64)
+        w1w_raw = keep.tile([P, 2 * H], U8, name="w1w_raw", align_bytes=64)
 
-        ws_raw = keep.tile([P, 2, H], U8, name="ws_raw", tag="late_old", align_bytes=64)
-        xs_win = keep.tile([P, T], U8, name="xs_win", tag="late_w3w", align_bytes=64)
-        xw_win = keep.tile([P, T], U32, name="xw_win", tag="late_w3s", align_bytes=64)
-        w2w_raw = keep.tile([P, 2 * H], U8, name="w2w_raw", tag="late_qa", align_bytes=64)
-        w1w_raw = keep.tile([P, 2 * H], U8, name="w1w_raw", tag="late_qb", align_bytes=64)
-
+        nc.vector.memset(ws_raw[:].bitcast(I32), 0)
         nc.vector.memset(xs_win[:, 0 : T // 2].bitcast(I32), 0)
         nc.gpsimd.memset(xs_win[:, T // 2 :].bitcast(I32), 0)
+
         warm = keep.tile([P, 1], F32, name="warm")
         warm_out = keep.tile([P, 1], F32, name="warm_out")
         nc.vector.memset(warm[:], 0.0)
         nc.scalar.activation(out=warm_out[:], in_=warm[:], func=ACT.Sigmoid)
 
-        nc.vector.memset(ws_raw[:].bitcast(I32), 0)
         ident = keep.tile([P, P], F32, name="ident")
         make_identity(nc, ident[:])
 
         nc.sync.dma_start(offs_t[:], offs)
         nc.sync.dma_start(out=w2w_raw[:].bitcast(I32), in_=w2_words[0].bitcast(I32))
         nc.sync.dma_start(out=w1w_raw[:].bitcast(I32), in_=w1_words[0].bitcast(I32))
-        load_scale_rows([nc.sync] * 4, xs_win[:], x_scales)
-        nc.sync.dma_start(out=xw_win[:].bitcast(I32), in_=x_words[0].rearrange("p n t -> p (n t)").bitcast(I32))
-        load_scale_rows([nc.sync] * 4, ws_raw[:, 0, :], w2_scales)
-        load_scale_rows([nc.sync] * 3 + [nc.scalar], ws_raw[:, 1, :], w1_scales)
         nc.sync.dma_start(pg_t[:], pg)
+        nc.sync.dma_start(out=ws_raw[0:P:SPREAD, 0, :].bitcast(I32), in_=w2_scales[0].bitcast(I32))
+        nc.sync.dma_start(out=ws_raw[0:P:SPREAD, 1, :].bitcast(I32), in_=w1_scales[0].bitcast(I32))
+        nc.sync.dma_start(out=xs_win[0:P:SPREAD, :].bitcast(I32), in_=x_scales[0].bitcast(I32))
+        nc.sync.dma_start(out=xw_win[:].bitcast(I32), in_=x_words[0].rearrange("p n t -> p (n t)").bitcast(I32))
+
+        def place_scale_rows(dst, src):
+            for r in range(1, 4):
+                nc.scalar.dma_start(out=dst[r:P:QUAD, :].bitcast(I32), in_=src[SPREAD * r : P : QUAD, :].bitcast(I32))
 
         def deal_words(raw, name):
-            dealt = keep.tile([P, PACK, 2 * P], U8, name=name, align_bytes=64)
+            dealt = keep.tile([P, PLANES, 2 * P], U8, name=name, align_bytes=64)
             nc.vector.tensor_copy(
                 out=dealt[:].rearrange("p t (m b) -> p t m b", b=2),
-                in_=raw[:].rearrange("p (m t b) -> p t m b", t=PACK, b=2),
+                in_=raw[:].rearrange("p (m t b) -> p t m b", t=PLANES, b=2),
             )
             return dealt
 
+        ws = keep.tile([P, 2, PLANES, P], U8, name="ws", align_bytes=64)
+        nc.vector.tensor_copy(out=ws[:], in_=ws_raw[:].rearrange("p w (m t) -> p w t m", t=PLANES))
+        ws_rows = ws[:].rearrange("p w t m -> p (w t m)")
+        place_scale_rows(ws_rows, ws_rows)
+        w2s, w1s = ws[:, 0], ws[:, 1]
+        xs_picked = keep.tile([P, S], U8, name="xs_picked", tag="then_qry_low", align_bytes=64)
+        nc.vector.tensor_copy(out=xs_picked[:], in_=xs_win[:].indirect(offs_t[:]))
+        xs = keep.tile([P, S], U8, name="xs", align_bytes=64)
+        nc.vector.tensor_copy(out=xs[:].bitcast(I32), in_=xs_picked[:].bitcast(I32))
+        place_scale_rows(xs[:], xs_picked[:])
         w2w = deal_words(w2w_raw, "w2w")
         w1w = deal_words(w1w_raw, "w1w")
-        xs = keep.tile([P, S], U8, name="xs", align_bytes=64)
-        nc.vector.tensor_copy(out=xs[:], in_=xs_win[:].indirect(offs_t[:]))
 
+        xw = []
+        for part, tag in enumerate(("then_w3s", "then_old")):
+            picked = keep.tile([P, BANK], U32, name="xw%d" % part, tag=tag, align_bytes=64)
+            columns = slice(part * BANK // PER_COLUMN, (part + 1) * BANK // PER_COLUMN)
+            nc.vector.tensor_copy(out=picked[:], in_=xw_win[:].indirect(offs_t[:, columns]))
+            xw.append(picked)
 
-        def gather_words(h, tag):
-            picked = keep.tile([P, BANK], U32, name="xw%d" % h, tag=tag, align_bytes=64)
-            nc.vector.tensor_copy(out=picked[:], in_=xw_win[:].indirect(offs_t[:, 32 * h : 32 * h + 32]))
-            return picked
-
-        xw = [gather_words(0, "xw0")]
-        ws = keep.tile([P, 2, PACK, P], U8, name="ws", align_bytes=64)
-        nc.vector.tensor_copy(out=ws[:], in_=ws_raw[:].rearrange("p w (m t) -> p w t m", t=PACK))
-        w2s, w1s = ws[:, 0], ws[:, 1]
-        xw.append(gather_words(1, "late_old"))
-
-        qry_v = qry.rearrange("(p t) r -> p t r", t=PACK)
-        q_first = keep.tile([P, 2 * U + PACK], F32, name="q_first", tag="late_qa", align_bytes=64)
-        q_second = keep.tile([P, 2 * U], F32, name="q_second", tag="late_qb", align_bytes=64)
-        nc.sync.dma_start(out=q_first[:, 0 : 2 * U].rearrange("p (t r) -> p t r", t=2), in_=qry_v[:, 0:2, :])
-        unit_t = q_first[:, 2 * U :]
-        nc.sync.dma_start(out=unit_t, in_=unit.rearrange("(p t) o -> p (t o)", t=PACK))
-        nc.sync.dma_start(out=q_second[:].rearrange("p (t r) -> p t r", t=2), in_=qry_v[:, 2:4, :])
-        q_tiles = [q_first, q_second]
-        w3w = keep.tile([P, 2 * N], U8, name="w3w", tag="late_w3w", align_bytes=64)
+        qry_planes = qry.rearrange("(p t) r -> p t r", t=PLANES)
+        qry_low = keep.tile([P, 2 * U + PLANES], F32, name="qry_low", tag="then_qry_low", align_bytes=64)
+        qry_high = keep.tile([P, 2 * U], F32, name="qry_high", tag="then_qry_high", align_bytes=64)
+        nc.sync.dma_start(out=qry_low[:, 0 : 2 * U].rearrange("p (t r) -> p t r", t=2), in_=qry_planes[:, 0:2, :])
+        unit_t = qry_low[:, 2 * U :]
+        nc.sync.dma_start(out=unit_t, in_=unit.rearrange("(p t) o -> p (t o)", t=PLANES))
+        nc.sync.dma_start(out=qry_high[:].rearrange("p (t r) -> p t r", t=2), in_=qry_planes[:, 2:4, :])
+        qry_tiles = [qry_low, qry_high]
+        w3w = keep.tile([P, 2 * N], U8, name="w3w", tag="then_w3w", align_bytes=64)
         nc.sync.dma_start(out=w3w[:].bitcast(I32), in_=w3_words[0].bitcast(I32))
-        w3s = keep.tile([P, N], U8, name="w3s", tag="late_w3s", align_bytes=64)
-        nc.vector.memset(w3s[:].bitcast(I32), 0)
-        load_scale_rows([nc.sync] * 4, w3s[:], w3_scales)
 
-        mt = keep.tile([P, PACK, U], F32, name="mt")
-        mean = keep.tile([P, PACK, U], F32, name="mean")
-        prods, wins, factors = {}, {}, {}
+        mt = keep.tile([P, PLANES, U], F32, name="mt")
+        mean = keep.tile([P, PLANES, U], F32, name="mean")
+        halves = [(0, HALF), (HALF, U)]
+        scores, windows, factors = {}, {}, {}
 
-        def product(words, scales, t, h, tag):
-            acc = psum.tile([P, BANK], F32, name=tag, tag=tag, bufs=3)
+        def product(words, scales, t, lo, hi, tag):
+            acc = psum.tile([P, hi - lo], F32, name=tag, tag=tag, bufs=3)
             nc.tensor.matmul_mx(
                 out=acc[:],
                 lhsT=words[:, t, :].bitcast(FP4X4),
                 lhsT_scale=scales[:, t, :],
-                rhs=xw[h][:].bitcast(FP8X4),
-                rhs_scale=xs[:, BANK * h : BANK * (h + 1)],
+                rhs=xw[lo // BANK][:, lo % BANK : lo % BANK + hi - lo].bitcast(FP8X4),
+                rhs_scale=xs[:, lo:hi],
                 start=True,
                 stop=True,
             )
             return acc
 
-        def score(t, h):
-            if h == 0:
-                prods[t] = ring.tile([P, S], F32, name="prod", bufs=3)
-            yw = product(w2w, w2s, t, h, "yw")
-            ys = product(w1w, w1s, t, h, "ys")
-            gate = ring.tile([P, BANK], F32, name="gate", bufs=3)
+        def score(t, lo, hi):
+            if lo == 0:
+                scores[t] = ring.tile([P, S], F32, name="sc", bufs=3)
+            yw = product(w2w, w2s, t, lo, hi, "yw")
+            ys = product(w1w, w1s, t, lo, hi, "ys")
+            gate = ring.tile([P, hi - lo], F32, name="gate", bufs=3)
             nc.scalar.activation(out=gate[:], in_=yw[:], func=ACT.Sigmoid)
             nc.vector.scalar_tensor_tensor(
-                out=prods[t][:, BANK * h : BANK * (h + 1)], in0=ys[:], scalar=0.0, in1=gate[:], op0=ALU.max, op1=ALU.mult
+                out=scores[t][:, lo:hi], in0=ys[:], scalar=0.0, in1=gate[:], op0=ALU.max, op1=ALU.mult
             )
 
         def factor(t):
-            th = ring.tile([P, U], F32, name="th")
-            nc.scalar.activation(out=th[:], in_=q_tiles[t // 2][:, (t % 2) * U : (t % 2 + 1) * U], func=ACT.Tanh)
+            bounded = ring.tile([P, U], F32, name="bounded")
+            nc.scalar.activation(out=bounded[:], in_=qry_tiles[t // 2][:, (t % 2) * U : (t % 2 + 1) * U], func=ACT.Tanh)
             factors[t] = ring.tile([P, U], F32, name="fac")
-            nc.scalar.activation(out=factors[t][:], in_=th[:], func=ACT.Copy, scale=unit_t[:, t : t + 1])
+            nc.scalar.activation(out=factors[t][:], in_=bounded[:], func=ACT.Copy, scale=unit_t[:, t : t + 1])
 
         def max_pairs(t):
-            wins[t] = ring.tile([P, V + 2 * V], F32, name="win", bufs=3)
-            quads = prods[t][:].rearrange("p (v d) -> p v d", d=D)
+            windows[t] = ring.tile([P, V + 2 * V], F32, name="window", bufs=3)
+            page = scores[t][:].rearrange("p (v d) -> p v d", d=D)
             nc.vector.tensor_tensor(
-                out=wins[t][:, V:].rearrange("p (v e) -> p v e", e=2), in0=quads[:, :, 0:2], in1=quads[:, :, 2:4], op=ALU.max
+                out=windows[t][:, V:].rearrange("p (v e) -> p v e", e=2), in0=page[:, :, 0:2], in1=page[:, :, 2:4], op=ALU.max
             )
 
         def max_final(t):
-            pairs = wins[t][:, V:].rearrange("p (v e) -> p v e", e=2)
-            nc.vector.tensor_tensor(out=wins[t][:, 0:V], in0=pairs[:, :, 0], in1=pairs[:, :, 1], op=ALU.max)
+            pairs = windows[t][:, V:].rearrange("p (v e) -> p v e", e=2)
+            nc.vector.tensor_tensor(out=windows[t][:, 0:V], in0=pairs[:, :, 0], in1=pairs[:, :, 1], op=ALU.max)
 
         def look_up(t, lo, hi):
-            nc.vector.tensor_tensor(
-                out=mt[:, t, lo:hi], in0=wins[t][:].indirect(pg_t[:, lo // 16 : hi // 16]), in1=factors[t][:, lo:hi], op=ALU.mult
-            )
+            pages = windows[t][:].indirect(pg_t[:, lo // PER_COLUMN : hi // PER_COLUMN])
+            nc.vector.tensor_tensor(out=mt[:, t, lo:hi], in0=pages, in1=factors[t][:, lo:hi], op=ALU.mult)
 
         def mean_by_transposes(t):
-            turned = psum.tile([P, P], F32, name="turned", tag="rr", bufs=2)
+            turned = psum.tile([P, P], F32, name="turned", tag="turn", bufs=2)
             members = mt[:, t, :].rearrange("p (g d) -> p d g", d=D)
             for d in range(D):
                 nc.tensor.matmul(
@@ -165,7 +167,7 @@ def tile_picked_yxindx_cent_p_kernel(
                 )
             mean_turned = ring.tile([P, P], F32, name="mean_turned")
             nc.scalar.activation(out=mean_turned[:], in_=turned[:], func=ACT.Copy, scale=1.0 / D)
-            back = psum.tile([P, P], F32, name="back", tag="rr", bufs=2)
+            back = psum.tile([P, P], F32, name="back", tag="turn", bufs=2)
             nc.tensor.transpose(back[:], mean_turned[:], ident[:])
             for lo, hi in halves:
                 nc.scalar.copy(
@@ -173,54 +175,65 @@ def tile_picked_yxindx_cent_p_kernel(
                     in_=back[:, lo // D : hi // D].unsqueeze(2).to_broadcast([P, HALF // D, D]),
                 )
 
-        last = PACK - 1
-        halves = [(h * HALF, (h + 1) * HALF) for h in range(2)]
-        score(0, 0)
-        score(1, 0)
-        score(0, 1)
-        score(1, 1)
+        score(0, 0, BANK // 2)
+        score(0, BANK // 2, BANK)
+        score(1, 0, BANK)
+        score(0, BANK, S)
+        score(1, BANK, S)
         max_pairs(0)
-        score(2, 0)
+        score(2, 0, BANK)
         factor(0)
         max_final(0)
         max_pairs(1)
         look_up(0, 0, U)
-        score(2, 1)
+        score(2, BANK, S)
         factor(1)
         mean_by_transposes(0)
         max_final(1)
         max_pairs(2)
         look_up(1, 0, U)
-        score(3, 0)
+        score(3, 0, BANK)
+
+        w3s = keep.tile([P, N], U8, name="w3s", tag="then_w3s", align_bytes=64)
+        nc.vector.memset(w3s[:].bitcast(I32), 0)
+        for r in range(4):
+            nc.sync.dma_start(out=w3s[r:P:QUAD, :].bitcast(I32), in_=w3_scales[0, r:16:4, :].bitcast(I32))
+
         factor(2)
         max_final(2)
-        score(3, 1)
+        score(3, BANK, S)
         mean_by_transposes(1)
         look_up(2, 0, U)
         mean_by_transposes(2)
         factor(3)
         max_pairs(3)
         max_final(3)
-        old_t = keep.tile([P, 2, U], F32, name="old_t", tag="late_old", align_bytes=64)
+
+        old_t = keep.tile([P, N // P, U], F32, name="old_t", tag="then_old", align_bytes=64)
         nc.sync.dma_start(out=old_t[:], in_=old.rearrange("(m p) r -> p m r", p=P))
+
+        last = PLANES - 1
         for lo, hi in halves:
             look_up(last, lo, hi)
-        sums = []
+        totals = []
         for lo, hi in halves:
             total = ring.tile([P, HALF // D], F32, name="total")
             nc.vector.tensor_reduce(
                 out=total[:], in_=mt[:, last, lo:hi].rearrange("p (g d) -> p g d", d=D), axis=mybir.AxisListType.X, op=ALU.add
             )
-            sums.append(total)
-        for h, (lo, hi) in enumerate(halves):
+            totals.append(total)
+        for total, (lo, hi) in zip(totals, halves):
             nc.vector.tensor_scalar(
                 out=mean[:, last, lo:hi].rearrange("p (g d) -> p g d", d=D),
-                in0=sums[h][:].unsqueeze(2).to_broadcast([P, HALF // D, D]),
-                scalar1=1.0 / D, scalar2=None, op0=ALU.mult,
+                in0=total[:].unsqueeze(2).to_broadcast([P, HALF // D, D]),
+                scalar1=1.0 / D,
+                scalar2=None,
+                op0=ALU.mult,
             )
+
         hids = []
-        for h, (lo, hi) in enumerate(halves):
-            hid = ring.tile([P, HALF, PACK], BF16, name="hid", align_bytes=64)
+        for lo, hi in halves:
+            hid = ring.tile([P, HALF, PLANES], BF16, name="hid", align_bytes=64)
             nc.vector.tensor_tensor(
                 out=hid[:].rearrange("p (c e) t -> p c t e", e=2),
                 in0=mt[:, :, lo:hi].rearrange("p t (c e) -> p c t e", e=2),
@@ -228,28 +241,28 @@ def tile_picked_yxindx_cent_p_kernel(
                 op=ALU.subtract,
             )
             hids.append(hid)
-        accs = []
-        for h in range(2):
+
+        blocks = []
+        for hid, (lo, hi) in zip(hids, halves):
             codes = ring.tile([P, HALF], U32, name="codes", align_bytes=64)
-            plane = ring.tile([P, HALF], U8, name="plane", align_bytes=64)
+            hid_scales = ring.tile([P, HALF], U8, name="hid_scales", align_bytes=64)
             nc.vector.quantize_mx(
-                out=codes[:].bitcast(FP8X4), scales=plane[:], in_=hids[h][:].rearrange("p r t -> p (r t)")
+                out=codes[:].bitcast(FP8X4), scales=hid_scales[:], in_=hid[:].rearrange("p r t -> p (r t)")
             )
             for m, tag in enumerate(("yw", "ys")):
-                acc = psum.tile([P, HALF], F32, name="rr", tag=tag, bufs=3)
+                rr = psum.tile([P, HALF], F32, name="rr", tag=tag, bufs=3)
                 nc.tensor.matmul_mx(
-                    out=acc[:],
+                    out=rr[:],
                     lhsT=w3w[:, 2 * P * m : 2 * P * (m + 1)].bitcast(FP4X4),
                     lhsT_scale=w3s[:, P * m : P * (m + 1)],
                     rhs=codes[:].bitcast(FP8X4),
-                    rhs_scale=plane[:],
+                    rhs_scale=hid_scales[:],
                     start=True,
                     stop=True,
                 )
-                accs.append((h, m, acc))
-        for h, m, acc in accs:
-            lo, hi = halves[h]
+                blocks.append((m, lo, hi, rr))
+        for m, lo, hi, rr in blocks:
             res = ring.tile([P, HALF], F32, name="res", bufs=4)
-            nc.vector.tensor_tensor(out=res[:], in0=acc[:], in1=old_t[:, m, lo:hi], op=ALU.add)
+            nc.vector.tensor_tensor(out=res[:], in0=rr[:], in1=old_t[:, m, lo:hi], op=ALU.add)
             queue = nc.sync if m == 0 else nc.scalar
             queue.dma_start(out=out[P * m : P * (m + 1), lo:hi], in_=res[:])

@@ -23,6 +23,7 @@ QUAD = 32
 SPREAD = 8
 BANK = 512
 HALF = U // 2
+BANKS = {"yw": 3, "ys": 3, "turn": 2}
 PER_COLUMN = 16
 
 
@@ -72,8 +73,7 @@ def tile_picked_yxindx_cent_p_kernel(
         def deal_words(raw, name):
             dealt = keep.tile([P, PLANES, 2 * P], U8, name=name, align_bytes=64)
             nc.vector.tensor_copy(
-                out=dealt[:].rearrange("p t (m b) -> p t m b", b=2),
-                in_=raw[:].rearrange("p (m t b) -> p t m b", t=PLANES, b=2),
+                out=dealt[:].bitcast(U16), in_=raw[:].bitcast(U16).rearrange("p (m t) -> p t m", t=PLANES),
             )
             return dealt
 
@@ -114,7 +114,7 @@ def tile_picked_yxindx_cent_p_kernel(
         scores, windows, factors = {}, {}, {}
 
         def product(words, scales, t, lo, hi, tag):
-            acc = psum.tile([P, hi - lo], F32, name=tag, tag=tag, bufs=3)
+            acc = psum.tile([P, hi - lo], F32, name=tag, tag=tag, bufs=BANKS[tag])
             nc.tensor.matmul_mx(
                 out=acc[:],
                 lhsT=words[:, t, :].bitcast(FP4X4),
@@ -131,7 +131,7 @@ def tile_picked_yxindx_cent_p_kernel(
                 scores[t] = ring.tile([P, S], F32, name="sc", bufs=3)
             yw = product(w2w, w2s, t, lo, hi, "yw")
             ys = product(w1w, w1s, t, lo, hi, "ys")
-            gate = ring.tile([P, hi - lo], F32, name="gate", bufs=3)
+            gate = ring.tile([P, hi - lo], F32, name="gate", bufs=2 * PLANES)
             nc.scalar.activation(out=gate[:], in_=yw[:], func=ACT.Sigmoid)
             nc.vector.scalar_tensor_tensor(
                 out=scores[t][:, lo:hi], in0=ys[:], scalar=0.0, in1=gate[:], op0=ALU.max, op1=ALU.mult
@@ -140,7 +140,7 @@ def tile_picked_yxindx_cent_p_kernel(
         def factor(t):
             bounded = ring.tile([P, U], F32, name="bounded")
             nc.scalar.activation(out=bounded[:], in_=qry_tiles[t // 2][:, (t % 2) * U : (t % 2 + 1) * U], func=ACT.Tanh)
-            factors[t] = ring.tile([P, U], F32, name="fac")
+            factors[t] = ring.tile([P, U], F32, name="fac", bufs=PLANES)
             nc.scalar.activation(out=factors[t][:], in_=bounded[:], func=ACT.Copy, scale=unit_t[:, t : t + 1])
 
         def max_pairs(t):
@@ -159,7 +159,7 @@ def tile_picked_yxindx_cent_p_kernel(
             nc.vector.tensor_tensor(out=mt[:, t, lo:hi], in0=pages, in1=factors[t][:, lo:hi], op=ALU.mult)
 
         def mean_by_transposes(t):
-            turned = psum.tile([P, P], F32, name="turned", tag="turn", bufs=2)
+            turned = psum.tile([P, P], F32, name="turned", tag="turn", bufs=BANKS["turn"])
             members = mt[:, t, :].rearrange("p (g d) -> p d g", d=D)
             for d in range(D):
                 nc.tensor.matmul(
@@ -167,7 +167,7 @@ def tile_picked_yxindx_cent_p_kernel(
                 )
             mean_turned = ring.tile([P, P], F32, name="mean_turned")
             nc.scalar.activation(out=mean_turned[:], in_=turned[:], func=ACT.Copy, scale=1.0 / D)
-            back = psum.tile([P, P], F32, name="back", tag="turn", bufs=2)
+            back = psum.tile([P, P], F32, name="back", tag="turn", bufs=BANKS["turn"])
             nc.tensor.transpose(back[:], mean_turned[:], ident[:])
             for lo, hi in halves:
                 nc.scalar.copy(
@@ -250,7 +250,7 @@ def tile_picked_yxindx_cent_p_kernel(
                 out=codes[:].bitcast(FP8X4), scales=hid_scales[:], in_=hid[:].rearrange("p r t -> p (r t)")
             )
             for m, tag in enumerate(("yw", "ys")):
-                rr = psum.tile([P, HALF], F32, name="rr", tag=tag, bufs=3)
+                rr = psum.tile([P, HALF], F32, name="rr", tag=tag, bufs=BANKS[tag])
                 nc.tensor.matmul_mx(
                     out=rr[:],
                     lhsT=w3w[:, 2 * P * m : 2 * P * (m + 1)].bitcast(FP4X4),

from contextlib import ExitStack

import concourse.mybir as mybir
from concourse.masks import make_identity

K, T, S, D, N, H, V, U = 512, 4096, 1024, 4, 256, 512, 256, 512
FLOPS = 2 * (2 * K * H * S + H * N * U)

F32 = mybir.dt.float32
BF16 = mybir.dt.bfloat16
I32 = mybir.dt.int32
U32 = mybir.dt.uint32
U16 = mybir.dt.uint16
U8 = mybir.dt.uint8
FP8X4 = mybir.dt.float8_e4m3fn_x4
FP4X4 = mybir.dt.float4_e2m1fn_x4
ACT = mybir.ActivationFunctionType
ALU = mybir.AluOpType

P = 128
PLANES = 4
QUAD = 32
SPREAD = 8
BANK = 512
HALF = U // 2
BANKS = {"yw": 3, "ys": 3, "turn": 2}
PER_COLUMN = 16


def tile_picked_yxindx_cent_p_kernel(
    tc, x_words, x_scales, w1_words, w1_scales, w2_words, w2_scales, qry, unit, w3_words, w3_scales, old, offs, pg, out
):
    nc = tc.nc
    with ExitStack() as ctx:
        lists = ctx.enter_context(tc.tile_pool(name="lists", bufs=1))
        keep = ctx.enter_context(tc.tile_pool(name="keep", bufs=1))
        ring = ctx.enter_context(tc.tile_pool(name="ring", bufs=2))
        psum = ctx.enter_context(tc.psum_pool(name="psum", bufs=1))

        offs_t = lists.tile([P, S // PER_COLUMN], U16, name="offs_t")
        pg_t = lists.tile([P, U // PER_COLUMN], U16, name="pg_t")
        ws_raw = keep.tile([P, 2, H], U8, name="ws_raw", tag="then_old", align_bytes=64)
        xs_win = keep.tile([P, T], U8, name="xs_win", align_bytes=64)
        xw_win = keep.tile([P, T], U32, name="xw_win", tag="then_qry_high", align_bytes=64)
        w2w_raw = keep.tile([P, 2 * H], U8, name="w2w_raw", tag="then_w3w", align_bytes=64)
        w1w_raw = keep.tile([P, 2 * H], U8, name="w1w_raw", align_bytes=64)

        nc.vector.memset(ws_raw[:].bitcast(I32), 0)
        nc.vector.memset(xs_win[:, 0 : T // 2].bitcast(I32), 0)
        nc.gpsimd.memset(xs_win[:, T // 2 :].bitcast(I32), 0)

        warm = keep.tile([P, 1], F32, name="warm")
        warm_out = keep.tile([P, 1], F32, name="warm_out")
        nc.vector.memset(warm[:], 0.0)
        nc.scalar.activation(out=warm_out[:], in_=warm[:], func=ACT.Sigmoid)

        ident = keep.tile([P, P], F32, name="ident")
        make_identity(nc, ident[:])

        nc.sync.dma_start(offs_t[:], offs)
        nc.sync.dma_start(out=w2w_raw[:].bitcast(I32), in_=w2_words[0].bitcast(I32))
        nc.sync.dma_start(out=w1w_raw[:].bitcast(I32), in_=w1_words[0].bitcast(I32))
        nc.sync.dma_start(pg_t[:], pg)
        nc.sync.dma_start(out=ws_raw[0:P:SPREAD, 0, :].bitcast(I32), in_=w2_scales[0].bitcast(I32))
        nc.sync.dma_start(out=ws_raw[0:P:SPREAD, 1, :].bitcast(I32), in_=w1_scales[0].bitcast(I32))
        nc.sync.dma_start(out=xs_win[0:P:SPREAD, :].bitcast(I32), in_=x_scales[0].bitcast(I32))
        nc.sync.dma_start(out=xw_win[:].bitcast(I32), in_=x_words[0].rearrange("p n t -> p (n t)").bitcast(I32))

        def place_scale_rows(dst, src):
            for r in range(1, 4):
                nc.scalar.dma_start(out=dst[r:P:QUAD, :].bitcast(I32), in_=src[SPREAD * r : P : QUAD, :].bitcast(I32))

        def deal_words(raw, name):
            dealt = keep.tile([P, PLANES, 2 * P], U8, name=name, align_bytes=64)
            nc.vector.tensor_copy(
                out=dealt[:].bitcast(U16), in_=raw[:].bitcast(U16).rearrange("p (m t) -> p t m", t=PLANES),
            )
            return dealt

        ws = keep.tile([P, 2, PLANES, P], U8, name="ws", align_bytes=64)
        nc.vector.tensor_copy(out=ws[:], in_=ws_raw[:].rearrange("p w (m t) -> p w t m", t=PLANES))
        ws_rows = ws[:].rearrange("p w t m -> p (w t m)")
        place_scale_rows(ws_rows, ws_rows)
        w2s, w1s = ws[:, 0], ws[:, 1]
        xs_picked = keep.tile([P, S], U8, name="xs_picked", tag="then_qry_low", align_bytes=64)
        nc.vector.tensor_copy(out=xs_picked[:], in_=xs_win[:].indirect(offs_t[:]))
        xs = keep.tile([P, S], U8, name="xs", align_bytes=64)
        nc.vector.tensor_copy(out=xs[:].bitcast(I32), in_=xs_picked[:].bitcast(I32))
        place_scale_rows(xs[:], xs_picked[:])
        w2w = deal_words(w2w_raw, "w2w")
        w1w = deal_words(w1w_raw, "w1w")

        xw = []
        for part, tag in enumerate(("then_w3s", "then_old")):
            picked = keep.tile([P, BANK], U32, name="xw%d" % part, tag=tag, align_bytes=64)
            columns = slice(part * BANK // PER_COLUMN, (part + 1) * BANK // PER_COLUMN)
            nc.vector.tensor_copy(out=picked[:], in_=xw_win[:].indirect(offs_t[:, columns]))
            xw.append(picked)

        qry_planes = qry.rearrange("(p t) r -> p t r", t=PLANES)
        qry_low = keep.tile([P, 2 * U + PLANES], F32, name="qry_low", tag="then_qry_low", align_bytes=64)
        qry_high = keep.tile([P, 2 * U], F32, name="qry_high", tag="then_qry_high", align_bytes=64)
        nc.sync.dma_start(out=qry_low[:, 0 : 2 * U].rearrange("p (t r) -> p t r", t=2), in_=qry_planes[:, 0:2, :])
        unit_t = qry_low[:, 2 * U :]
        nc.sync.dma_start(out=unit_t, in_=unit.rearrange("(p t) o -> p (t o)", t=PLANES))
        nc.sync.dma_start(out=qry_high[:].rearrange("p (t r) -> p t r", t=2), in_=qry_planes[:, 2:4, :])
        qry_tiles = [qry_low, qry_high]
        w3w = keep.tile([P, 2 * N], U8, name="w3w", tag="then_w3w", align_bytes=64)
        nc.sync.dma_start(out=w3w[:].bitcast(I32), in_=w3_words[0].bitcast(I32))

        mt = keep.tile([P, PLANES, U], F32, name="mt")
        mean = keep.tile([P, PLANES, U], F32, name="mean")
        halves = [(0, HALF), (HALF, U)]
        scores, windows, factors = {}, {}, {}

        def product(words, scales, t, lo, hi, tag):
            acc = psum.tile([P, hi - lo], F32, name=tag, tag=tag, bufs=BANKS[tag])
            nc.tensor.matmul_mx(
                out=acc[:],
                lhsT=words[:, t, :].bitcast(FP4X4),
                lhsT_scale=scales[:, t, :],
                rhs=xw[lo // BANK][:, lo % BANK : lo % BANK + hi - lo].bitcast(FP8X4),
                rhs_scale=xs[:, lo:hi],
                start=True,
                stop=True,
            )
            return acc

        def score(t, lo, hi):
            if lo == 0:
                scores[t] = ring.tile([P, S], F32, name="sc", bufs=3)
            yw = product(w2w, w2s, t, lo, hi, "yw")
            ys = product(w1w, w1s, t, lo, hi, "ys")
            gate = ring.tile([P, hi - lo], F32, name="gate", bufs=2 * PLANES)
            nc.scalar.activation(out=gate[:], in_=yw[:], func=ACT.Sigmoid)
            nc.vector.scalar_tensor_tensor(
                out=scores[t][:, lo:hi], in0=ys[:], scalar=0.0, in1=gate[:], op0=ALU.max, op1=ALU.mult
            )

        def factor(t):
            bounded = ring.tile([P, U], F32, name="bounded")
            nc.scalar.activation(out=bounded[:], in_=qry_tiles[t // 2][:, (t % 2) * U : (t % 2 + 1) * U], func=ACT.Tanh)
            factors[t] = ring.tile([P, U], F32, name="fac", bufs=PLANES)
            nc.scalar.activation(out=factors[t][:], in_=bounded[:], func=ACT.Copy, scale=unit_t[:, t : t + 1])

        def max_pairs(t):
            windows[t] = ring.tile([P, V + 2 * V], F32, name="window", bufs=3)
            page = scores[t][:].rearrange("p (v d) -> p v d", d=D)
            nc.vector.tensor_tensor(
                out=windows[t][:, V:].rearrange("p (v e) -> p v e", e=2), in0=page[:, :, 0:2], in1=page[:, :, 2:4], op=ALU.max
            )

        def max_final(t):
            pairs = windows[t][:, V:].rearrange("p (v e) -> p v e", e=2)
            nc.vector.tensor_tensor(out=windows[t][:, 0:V], in0=pairs[:, :, 0], in1=pairs[:, :, 1], op=ALU.max)

        def look_up(t, lo, hi):
            pages = windows[t][:].indirect(pg_t[:, lo // PER_COLUMN : hi // PER_COLUMN])
            nc.vector.tensor_tensor(out=mt[:, t, lo:hi], in0=pages, in1=factors[t][:, lo:hi], op=ALU.mult)

        def mean_by_transposes(t):
            turned = psum.tile([P, P], F32, name="turned", tag="turn", bufs=BANKS["turn"])
            members = mt[:, t, :].rearrange("p (g d) -> p d g", d=D)
            for d in range(D):
                nc.tensor.matmul(
                    out=turned[:], lhsT=members[:, d, :], rhs=ident[:], is_transpose=True, start=(d == 0), stop=(d == D - 1)
                )
            mean_turned = ring.tile([P, P], F32, name="mean_turned")
            nc.scalar.activation(out=mean_turned[:], in_=turned[:], func=ACT.Copy, scale=1.0 / D)
            back = psum.tile([P, P], F32, name="back", tag="turn", bufs=BANKS["turn"])
            nc.tensor.transpose(back[:], mean_turned[:], ident[:])
            for lo, hi in halves:
                nc.scalar.copy(
                    out=mean[:, t, lo:hi].rearrange("p (g d) -> p g d", d=D),
                    in_=back[:, lo // D : hi // D].unsqueeze(2).to_broadcast([P, HALF // D, D]),
                )

        score(0, 0, BANK // 2)
        score(0, BANK // 2, BANK)
        score(1, 0, BANK)
        score(0, BANK, S)
        score(1, BANK, S)
        max_pairs(0)
        score(2, 0, BANK)
        factor(0)
        max_final(0)
        max_pairs(1)
        look_up(0, 0, U)
        score(2, BANK, S)
        factor(1)
        mean_by_transposes(0)
        max_final(1)
        max_pairs(2)
        look_up(1, 0, U)
        score(3, 0, BANK)

        w3s = keep.tile([P, N], U8, name="w3s", tag="then_w3s", align_bytes=64)
        nc.vector.memset(w3s[:].bitcast(I32), 0)
        for r in range(4):
            nc.sync.dma_start(out=w3s[r:P:QUAD, :].bitcast(I32), in_=w3_scales[0, r:16:4, :].bitcast(I32))

        factor(2)
        max_final(2)
        score(3, BANK, S)
        mean_by_transposes(1)
        look_up(2, 0, U)
        mean_by_transposes(2)
        factor(3)
        max_pairs(3)
        max_final(3)

        old_t = keep.tile([P, N // P, U], F32, name="old_t", tag="then_old", align_bytes=64)
        nc.sync.dma_start(out=old_t[:], in_=old.rearrange("(m p) r -> p m r", p=P))

        last = PLANES - 1
        for lo, hi in halves:
            look_up(last, lo, hi)
        totals = []
        for lo, hi in halves:
            total = ring.tile([P, HALF // D], F32, name="total")
            nc.vector.tensor_reduce(
                out=total[:], in_=mt[:, last, lo:hi].rearrange("p (g d) -> p g d", d=D), axis=mybir.AxisListType.X, op=ALU.add
            )
            totals.append(total)
        for total, (lo, hi) in zip(totals, halves):
            nc.vector.tensor_scalar(
                out=mean[:, last, lo:hi].rearrange("p (g d) -> p g d", d=D),
                in0=total[:].unsqueeze(2).to_broadcast([P, HALF // D, D]),
                scalar1=1.0 / D,
                scalar2=None,
                op0=ALU.mult,
            )

        hids = []
        for lo, hi in halves:
            hid = ring.tile([P, HALF, PLANES], BF16, name="hid", align_bytes=64)
            nc.vector.tensor_tensor(
                out=hid[:].rearrange("p (c e) t -> p c t e", e=2),
                in0=mt[:, :, lo:hi].rearrange("p t (c e) -> p c t e", e=2),
                in1=mean[:, :, lo:hi].rearrange("p t (c e) -> p c t e", e=2),
                op=ALU.subtract,
            )
            hids.append(hid)

        blocks = []
        for hid, (lo, hi) in zip(hids, halves):
            codes = ring.tile([P, HALF], U32, name="codes", align_bytes=64)
            hid_scales = ring.tile([P, HALF], U8, name="hid_scales", align_bytes=64)
            nc.vector.quantize_mx(
                out=codes[:].bitcast(FP8X4), scales=hid_scales[:], in_=hid[:].rearrange("p r t -> p (r t)")
            )
            for m, tag in enumerate(("yw", "ys")):
                rr = psum.tile([P, HALF], F32, name="rr", tag=tag, bufs=BANKS[tag])
                nc.tensor.matmul_mx(
                    out=rr[:],
                    lhsT=w3w[:, 2 * P * m : 2 * P * (m + 1)].bitcast(FP4X4),
                    lhsT_scale=w3s[:, P * m : P * (m + 1)],
                    rhs=codes[:].bitcast(FP8X4),
                    rhs_scale=hid_scales[:],
                    start=True,
                    stop=True,
                )
                blocks.append((m, lo, hi, rr))
        for m, lo, hi, rr in blocks:
            res = ring.tile([P, HALF], F32, name="res", bufs=4)
            nc.vector.tensor_tensor(out=res[:], in0=rr[:], in1=old_t[:, m, lo:hi], op=ALU.add)
            queue = nc.sync if m == 0 else nc.scalar
            queue.dma_start(out=out[P * m : P * (m + 1), lo:hi], in_=res[:])
